import numpy as np
import ml_dtypes


def mxq(x, axis, fmt="e4m3"):
    dtype, down = {"e4m3": (ml_dtypes.float8_e4m3fn, 7), "e5m2": (ml_dtypes.float8_e5m2, 14)}[fmt]
    v = np.moveaxis(np.asarray(x, np.float32).astype(ml_dtypes.bfloat16).astype(np.float64), axis, -1)
    blocks = v.reshape(v.shape[:-1] + (-1, 32))
    amax = np.abs(blocks).max(-1, keepdims=True)
    byte = np.maximum(np.where(amax > 0, np.frexp(amax)[1] - 1 + 127, 0) - down, 1)
    scale = np.exp2(byte - 127.0)
    codes = (blocks / scale).astype(np.float32).astype(dtype).astype(np.float64)
    return np.moveaxis((codes * scale).reshape(v.shape), -1, axis)


WIDE = False


def mx_kscale(k):
    if not WIDE:
        return np.ones(k)
    levels = np.array([10, -10, 5, -5, 0])
    if k % 512:
        return np.exp2(np.random.permutation(np.resize(levels, k // 32))).repeat(32)
    a = np.empty((k // 512, 16))
    for p in range(k // 512):
        a[p, :8] = np.random.permutation(np.resize(levels, 8))
        for g in range(8):
            far = levels[np.abs(levels - a[p, g]) >= 10]
            a[p, g + 8] = far[np.random.randint(len(far))]
    return np.exp2(a.ravel()).repeat(32)


def f64(x):
    return np.asarray(x).astype(np.float64)


def striped(idx):
    return np.tile(np.asarray(idx).reshape(-1, 16).T, (8, 1)).astype(np.uint16)


def unstriped(offs):
    return offs[:16].T.reshape(-1).astype(np.int64)


def striped8(idx):
    return np.asarray(idx).reshape(8, -1, 16).transpose(0, 2, 1).reshape(128, -1).astype(np.uint16)


def unstriped8(offs):
    return offs.reshape(8, 16, -1).transpose(0, 2, 1).reshape(8, -1).astype(np.int64)


def pick8(x, idx, run):
    r = np.arange(len(x))
    return x[r[:, None], idx[r % (8 * run) // run]]


E2M1 = np.array([0.0, 0.5, 1.0, 1.5, 2.0, 3.0, 4.0, 6.0, -0.0, -0.5, -1.0, -1.5, -2.0, -3.0, -4.0, -6.0])


def pack_weight(w, fmt):
    k, n = w.shape
    w = f64(np.asarray(w, np.float32).astype(ml_dtypes.bfloat16)).reshape(k // 32, 32, n)
    amax = np.abs(w).max(1)
    if fmt == "e4m3":
        byte = np.frexp(amax)[1] - 1 + 127 - 7
    else:
        mant, ex = np.frexp(amax / 6.0)
        byte = np.where(mant > 0.5, ex, ex - 1) + 127
    byte = np.clip(np.where(amax > 0, byte, 1), 1, 254)
    scaled = (w * np.exp2(127.0 - byte)[:, None, :]).reshape(k, n).astype(np.float32)
    by_word = np.ascontiguousarray(scaled.reshape(k // 512, 128, 4, n).transpose(0, 1, 3, 2))
    if fmt == "e4m3":
        words = by_word.astype(ml_dtypes.float8_e4m3fn).view(np.uint8)
    else:
        c = by_word.astype(ml_dtypes.float4_e2m1fn).view(np.uint8) & 0xF
        words = (c[..., 0::2] | (c[..., 1::2] << 4)).reshape(k // 512, 128, 2 * n)
    return np.ascontiguousarray(words), np.ascontiguousarray(byte.astype(np.uint8).reshape(k // 512, 16, n))


def unpack_weight(words, scales, fmt):
    g, _, n = scales.shape
    words = np.ascontiguousarray(words).reshape(g, 128, n, -1)
    if fmt == "e4m3":
        vals = words.view(ml_dtypes.float8_e4m3fn).astype(np.float64)
    else:
        nib = np.empty((g, 128, n, 4), np.uint8)
        nib[..., 0::2] = words & 0xF
        nib[..., 1::2] = words >> 4
        vals = E2M1[nib]
    vals = vals * np.repeat(np.exp2(scales.astype(np.float64) - 127.0), 8, axis=1)[..., None]
    return vals.transpose(0, 1, 3, 2).reshape(g * 512, n)


K, T, J, R, V, C, N = 512, 1024, 256, 512, 1024, 512, 256


def setup_inputs():
    n = np.random.standard_normal
    idx = np.random.permutation(V)[:R]
    idx2 = np.random.permutation(T)[:J]
    idx3 = np.stack([np.random.permutation(C)[:J] for _ in range(8)])
    idx4 = np.random.permutation(C)[:J]
    idx5 = np.random.permutation(C)[:J]
    fk = mx_kscale(K)
    fr = mx_kscale(R)
    tr = np.ones(V)
    tr[idx] = fr
    xtp = pack_weight(n((K, T)) / fk[:, None], "e2m1")
    wtp = pack_weight(n((K, V)) * 1 / np.sqrt(K) * fk[:, None] * tr, "e4m3")
    wbp = pack_weight(n((R, N)) * 1 / np.sqrt(R) / fr[:, None], "e2m1")
    return {
        "xt_words": xtp[0],
        "xt_scales": xtp[1],
        "wt_words": wtp[0],
        "wt_scales": wtp[1],
        "wb_words": wbp[0],
        "wb_scales": wbp[1],
        "offs": striped(idx),
        "offs2": striped(idx2),
        "offs3": striped8(idx3),
        "offs4": striped(idx4),
        "offs5": striped(idx5),
    }


def reference(xt_words, xt_scales, wt_words, wt_scales, wb_words, wb_scales, offs, offs2, offs3, offs4, offs5):
    idx = unstriped(offs)
    idx2 = unstriped(offs2)
    idx3 = unstriped8(offs3)
    idx4 = unstriped(offs4)
    idx5 = unstriped(offs5)
    xtu = unpack_weight(xt_words, xt_scales, "e2m1")
    wtu = unpack_weight(wt_words, wt_scales, "e4m3")
    wbu = unpack_weight(wb_words, wb_scales, "e2m1")
    wtidxg = wtu[:, idx]
    xtidx2g = xtu[:, idx2]
    a = wtidxg.T @ xtidx2g
    pa = np.zeros((R, C))
    pa[np.arange(R)[:, None], idx3[np.arange(R) % 512 // 64]] = a
    hid = np.minimum(np.abs(pa[:, idx4] - a), np.abs(pa[:, idx5] - a))
    hidq = mxq(hid, 0, "e4m3")
    p = wbu.T @ hidq
    return p

@@ -1,0 +1,134 @@
+from contextlib import ExitStack
+
+import concourse.mybir as mybir
+
+K, T, J, R, V, C, N = 512, 1024, 256, 512, 1024, 512, 256
+FLOPS = 2 * K * R * J + 2 * R * N * J
+
+F32 = mybir.dt.float32
+BF16 = mybir.dt.bfloat16
+I32 = mybir.dt.int32
+U32 = mybir.dt.uint32
+U16 = mybir.dt.uint16
+U8 = mybir.dt.uint8
+FP8X4 = mybir.dt.float8_e4m3fn_x4
+FP4X4 = mybir.dt.float4_e2m1fn_x4
+ALU = mybir.AluOpType
+ACT = mybir.ActivationFunctionType
+
+P = 128
+PACK = 4
+HALF = J // 2
+GROUP = 16
+
+
+def tile_list_nearerpost_kernel(tc, xt_words, xt_scales, wt_words, wt_scales, wb_words, wb_scales,
+                                   offs, offs2, offs3, offs4, offs5, out):
+    nc = tc.nc
+    with ExitStack() as ctx:
+        sb = ctx.enter_context(tc.tile_pool(name="sb", bufs=1))
+        ps = ctx.enter_context(tc.psum_pool(name="ps", bufs=1))
+
+        def half_cols(h):
+            return slice(h * HALF, (h + 1) * HALF)
+
+        def half_list(tile, h):
+            return tile[:, h * HALF // GROUP : (h + 1) * HALF // GROUP]
+
+        def load_plane(plane, rows):
+            for q in range(4):
+                nc.sync.dma_start(plane[32 * q : 32 * q + 4, :].bitcast(I32), rows[0, 4 * q : 4 * q + 4, :].bitcast(I32))
+
+        l1 = sb.tile([P, R // GROUP], U16, name="l1")
+        l2 = sb.tile([P, J // GROUP], U16, name="l2")
+        l3 = sb.tile([P, J // GROUP], U16, name="l3")
+        l4 = sb.tile([P, J // GROUP], U16, name="l4")
+        l5 = sb.tile([P, J // GROUP], U16, name="l5")
+        wt_w = sb.tile([P, V], U32, name="wt_w", align_bytes=64)
+        wt_s = sb.tile([P, V], U8, name="wt_s", align_bytes=64)
+        xt_w = sb.tile([P, T], U16, name="xt_w", align_bytes=64)
+        xt_s = sb.tile([P, T], U8, name="xt_s", align_bytes=64)
+        wb_w = sb.tile([P, N], U16, name="wb_w", align_bytes=64)
+        wb_s = sb.tile([P, N], U8, name="wb_s", align_bytes=64)
+        board = [sb.tile([P, C], F32, name="board%d" % t) for t in range(PACK)]
+
+        for plane in (wt_s, xt_s, wb_s):
+            nc.vector.memset(plane[:].bitcast(I32), 0)
+        nc.sync.dma_start(l1[:], offs)
+        nc.sync.dma_start(wt_w[:].bitcast(I32), wt_words[0].rearrange("p c r -> p (c r)").bitcast(I32))
+        nc.sync.dma_start(l2[:], offs2)
+        nc.sync.dma_start(xt_w[:].bitcast(I32), xt_words[0].bitcast(I32))
+        load_plane(wt_s, wt_scales)
+        load_plane(xt_s, xt_scales)
+        nc.sync.dma_start(l3[:], offs3)
+        nc.sync.dma_start(l4[:], offs4)
+        nc.sync.dma_start(l5[:], offs5)
+        nc.sync.dma_start(wb_w[:].bitcast(I32), wb_words[0].bitcast(I32))
+        load_plane(wb_s, wb_scales)
+        for t in range(PACK):
+            nc.vector.memset(board[t][:], 0.0)
+
+        gw_w = sb.tile([P, R], U32, name="gw_w", align_bytes=64)
+        gw_s = sb.tile([P, R], U8, name="gw_s", align_bytes=64)
+        gx_w = sb.tile([P, J], U16, name="gx_w", align_bytes=64)
+        gx_s = sb.tile([P, J], U8, name="gx_s", align_bytes=64)
+
+        def gather_x(h):
+            nc.vector.tensor_copy(gx_w[:, half_cols(h)], xt_w[:].indirect(half_list(l2, h)))
+            nc.vector.tensor_copy(gx_s[:, half_cols(h)], xt_s[:].indirect(half_list(l2, h)))
+
+        nc.vector.tensor_copy(gw_w[:].rearrange("p (t q) -> p q t", t=PACK), wt_w[:].indirect(l1[:]))
+        nc.vector.tensor_copy(gw_s[:].rearrange("p (t q) -> p q t", t=PACK), wt_s[:].indirect(l1[:]))
+        gather_x(0)
+
+        def first_product(acc, t, cols):
+            rows = slice(t * P, (t + 1) * P)
+            nc.tensor.matmul_mx(out=acc, lhsT=gw_w[:, rows].bitcast(FP8X4), lhsT_scale=gw_s[:, rows],
+                                rhs=gx_w[:, cols].bitcast(FP4X4), rhs_scale=gx_s[:, cols], start=True, stop=True)
+
+        a = [sb.tile([P, J], F32, name="a%d" % t) for t in range(PACK)]
+        acc00 = ps.tile([P, HALF], F32, name="acc00")
+        first_product(acc00[:], 0, half_cols(0))
+        nc.scalar.copy(a[0][:, half_cols(0)], acc00[:])
+        nc.scalar.activation(board[0][:].indirect(half_list(l3, 0)), a[0][:, half_cols(0)], ACT.Copy)
+        gather_x(1)
+        acc01 = ps.tile([P, HALF], F32, name="acc01")
+        first_product(acc01[:], 0, half_cols(1))
+        nc.vector.tensor_copy(a[0][:, half_cols(1)], acc01[:])
+        nc.scalar.activation(board[0][:].indirect(half_list(l3, 1)), a[0][:, half_cols(1)], ACT.Copy)
+        for t in range(1, PACK):
+            acc = ps.tile([P, J], F32, name="acc%d" % t)
+            first_product(acc[:], t, slice(0, J))
+            nc.vector.tensor_copy(a[t][:], acc[:])
+            nc.scalar.activation(board[t][:].indirect(l3[:]), a[t][:], ACT.Copy)
+
+        diff = [sb.tile([P, 2, 2, J], F32, name="diff%d" % u) for u in range(2)]
+        mag = sb.tile([P, 2, 2, J, 2], F32, name="mag")
+        for t in range(PACK - 1):
+            for w, lst in enumerate((l4, l5)):
+                nc.vector.tensor_tensor(diff[t // 2][:, w, t % 2, :], board[t][:].indirect(lst[:]), a[t][:], ALU.subtract)
+        nc.scalar.activation(mag[:, 0], diff[0][:].rearrange("p w e j -> p w j e"), ACT.Abs)
+        last = PACK - 1
+        for h in range(2):
+            for w, lst in enumerate((l4, l5)):
+                nc.vector.tensor_tensor(diff[1][:, w, 1, half_cols(h)], board[last][:].indirect(half_list(lst, h)),
+                                        a[last][:, half_cols(h)], ALU.subtract)
+        for h in range(2):
+            nc.scalar.activation(mag[:, 1, :, half_cols(h), :],
+                                 diff[1][:, :, :, half_cols(h)].rearrange("p w e j -> p w j e"), ACT.Abs)
+
+        for h in range(2):
+            hid = sb.tile([P, HALF, 2, 2], BF16, name="hid%d" % h, align_bytes=64)
+            nc.vector.tensor_tensor(hid[:], mag[:, :, 0, half_cols(h), :].rearrange("p u j e -> p j u e"),
+                                    mag[:, :, 1, half_cols(h), :].rearrange("p u j e -> p j u e"), ALU.min)
+            codes = sb.tile([P, HALF], U32, name="codes%d" % h, align_bytes=64)
+            scales = sb.tile([P, HALF], U8, name="scales%d" % h, align_bytes=64)
+            nc.vector.quantize_mx(out=codes[:].bitcast(FP8X4), scales=scales[:], in_=hid[:].rearrange("p j u e -> p (j u e)"))
+            res_ps = ps.tile([P, N // P, HALF], F32, name="res_ps%d" % h)
+            for m in range(N // P):
+                cols = slice(m * P, (m + 1) * P)
+                nc.tensor.matmul_mx(out=res_ps[:, m, :], lhsT=wb_w[:, cols].bitcast(FP4X4), lhsT_scale=wb_s[:, cols],
+                                    rhs=codes[:].bitcast(FP8X4), rhs_scale=scales[:], start=True, stop=True)
+            res = sb.tile([P, N // P, HALF], F32, name="res%d" % h)
+            nc.scalar.copy(res[:], res_ps[:])
+            nc.sync.dma_start(out[:, half_cols(h)].rearrange("(m p) j -> p m j", p=P), res[:])

@@ -55,7 +55,7 @@ def tile_list_nearerpost_kernel(tc, xt_words, xt_scales, wt_words, wt_scales, wb
         for plane in (wt_s, xt_s, wb_s):
             nc.vector.memset(plane[:].bitcast(I32), 0)
         nc.sync.dma_start(l1[:], offs)
-        nc.sync.dma_start(wt_w[:].bitcast(I32), wt_words[0].rearrange("p c r -> p (c r)").bitcast(I32))
+        nc.scalar.dma_start(wt_w[:].bitcast(I32), wt_words[0].rearrange("p c r -> p (c r)").bitcast(I32))
         nc.sync.dma_start(l2[:], offs2)
         nc.sync.dma_start(xt_w[:].bitcast(I32), xt_words[0].bitcast(I32))
         load_plane(wt_s, wt_scales)
@@ -66,7 +66,7 @@ def tile_list_nearerpost_kernel(tc, xt_words, xt_scales, wt_words, wt_scales, wb
         nc.sync.dma_start(wb_w[:].bitcast(I32), wb_words[0].bitcast(I32))
         load_plane(wb_s, wb_scales)
         for t in range(PACK):
-            nc.vector.memset(board[t][:], 0.0)
+            (nc.vector if t < 2 else nc.gpsimd).memset(board[t][:], 0.0)
 
         gw_w = sb.tile([P, R], U32, name="gw_w", align_bytes=64)
         gw_s = sb.tile([P, R], U8, name="gw_s", align_bytes=64)
@@ -102,7 +102,7 @@ def tile_list_nearerpost_kernel(tc, xt_words, xt_scales, wt_words, wt_scales, wb
             nc.vector.tensor_copy(a[t][:], acc[:])
             nc.scalar.activation(board[t][:].indirect(l3[:]), a[t][:], ACT.Copy)
 
-        diff = [sb.tile([P, 2, 2, J], F32, name="diff%d" % u) for u in range(2)]
+        diff = [sb.tile([P, 2, 2, J], F32, name="diff0", tag="gw_w", align_bytes=64), sb.tile([P, 2, 2, J], F32, name="diff1")]
         mag = sb.tile([P, 2, 2, J, 2], F32, name="mag")
         for t in range(PACK - 1):
             for w, lst in enumerate((l4, l5)):
@@ -124,11 +124,14 @@ def tile_list_nearerpost_kernel(tc, xt_words, xt_scales, wt_words, wt_scales, wb
             codes = sb.tile([P, HALF], U32, name="codes%d" % h, align_bytes=64)
             scales = sb.tile([P, HALF], U8, name="scales%d" % h, align_bytes=64)
             nc.vector.quantize_mx(out=codes[:].bitcast(FP8X4), scales=scales[:], in_=hid[:].rearrange("p j u e -> p (j u e)"))
-            res_ps = ps.tile([P, N // P, HALF], F32, name="res_ps%d" % h)
             for m in range(N // P):
-                cols = slice(m * P, (m + 1) * P)
-                nc.tensor.matmul_mx(out=res_ps[:, m, :], lhsT=wb_w[:, cols].bitcast(FP4X4), lhsT_scale=wb_s[:, cols],
+                rows = slice(m * P, (m + 1) * P)
+                res_ps = ps.tile([P, HALF], F32, name="res_ps%d%d" % (h, m), tag="res_ps%d" % m if h == 1 else "acc0%d" % m)
+                nc.tensor.matmul_mx(out=res_ps[:], lhsT=wb_w[:, rows].bitcast(FP4X4), lhsT_scale=wb_s[:, rows],
                                     rhs=codes[:].bitcast(FP8X4), rhs_scale=scales[:], start=True, stop=True)
-            res = sb.tile([P, N // P, HALF], F32, name="res%d" % h)
-            nc.scalar.copy(res[:], res_ps[:])
-            nc.sync.dma_start(out[:, half_cols(h)].rearrange("(m p) j -> p m j", p=P), res[:])
+                res = sb.tile([P, HALF], F32, name="res%d%d" % (h, m))
+                if h == 1 and m == 1:
+                    nc.vector.tensor_copy(res[:], res_ps[:])
+                else:
+                    nc.scalar.copy(res[:], res_ps[:])
+                nc.sync.dma_start(out[rows, half_cols(h)], res[:])

from contextlib import ExitStack

import concourse.mybir as mybir

K, T, J, R, V, C, N = 512, 1024, 256, 512, 1024, 512, 256
FLOPS = 2 * K * R * J + 2 * R * N * J

F32 = mybir.dt.float32
BF16 = mybir.dt.bfloat16
I32 = mybir.dt.int32
U32 = mybir.dt.uint32
U16 = mybir.dt.uint16
U8 = mybir.dt.uint8
FP8X4 = mybir.dt.float8_e4m3fn_x4
FP4X4 = mybir.dt.float4_e2m1fn_x4
ALU = mybir.AluOpType
ACT = mybir.ActivationFunctionType

P = 128
PACK = 4
HALF = J // 2
GROUP = 16


def tile_list_nearerpost_kernel(tc, xt_words, xt_scales, wt_words, wt_scales, wb_words, wb_scales,
                                   offs, offs2, offs3, offs4, offs5, out):
    nc = tc.nc
    with ExitStack() as ctx:
        sb = ctx.enter_context(tc.tile_pool(name="sb", bufs=1))
        ps = ctx.enter_context(tc.psum_pool(name="ps", bufs=1))

        def half_cols(h):
            return slice(h * HALF, (h + 1) * HALF)

        def half_list(tile, h):
            return tile[:, h * HALF // GROUP : (h + 1) * HALF // GROUP]

        def load_plane(plane, rows):
            for q in range(4):
                nc.sync.dma_start(plane[32 * q : 32 * q + 4, :].bitcast(I32), rows[0, 4 * q : 4 * q + 4, :].bitcast(I32))

        l1 = sb.tile([P, R // GROUP], U16, name="l1")
        l2 = sb.tile([P, J // GROUP], U16, name="l2")
        l3 = sb.tile([P, J // GROUP], U16, name="l3")
        l4 = sb.tile([P, J // GROUP], U16, name="l4")
        l5 = sb.tile([P, J // GROUP], U16, name="l5")
        wt_w = sb.tile([P, V], U32, name="wt_w", align_bytes=64)
        wt_s = sb.tile([P, V], U8, name="wt_s", align_bytes=64)
        xt_w = sb.tile([P, T], U16, name="xt_w", align_bytes=64)
        xt_s = sb.tile([P, T], U8, name="xt_s", align_bytes=64)
        wb_w = sb.tile([P, N], U16, name="wb_w", align_bytes=64)
        wb_s = sb.tile([P, N], U8, name="wb_s", align_bytes=64)
        board = [sb.tile([P, C], F32, name="board%d" % t) for t in range(PACK)]

        for plane in (wt_s, xt_s, wb_s):
            nc.vector.memset(plane[:].bitcast(I32), 0)
        nc.sync.dma_start(l1[:], offs)
        nc.scalar.dma_start(wt_w[:].bitcast(I32), wt_words[0].rearrange("p c r -> p (c r)").bitcast(I32))
        nc.sync.dma_start(l2[:], offs2)
        nc.sync.dma_start(xt_w[:].bitcast(I32), xt_words[0].bitcast(I32))
        load_plane(wt_s, wt_scales)
        load_plane(xt_s, xt_scales)
        nc.sync.dma_start(l3[:], offs3)
        nc.sync.dma_start(l4[:], offs4)
        nc.sync.dma_start(l5[:], offs5)
        nc.sync.dma_start(wb_w[:].bitcast(I32), wb_words[0].bitcast(I32))
        load_plane(wb_s, wb_scales)
        for t in range(PACK):
            (nc.vector if t < 2 else nc.gpsimd).memset(board[t][:], 0.0)

        gw_w = sb.tile([P, R], U32, name="gw_w", align_bytes=64)
        gw_s = sb.tile([P, R], U8, name="gw_s", align_bytes=64)
        gx_w = sb.tile([P, J], U16, name="gx_w", align_bytes=64)
        gx_s = sb.tile([P, J], U8, name="gx_s", align_bytes=64)

        def gather_x(h):
            nc.vector.tensor_copy(gx_w[:, half_cols(h)], xt_w[:].indirect(half_list(l2, h)))
            nc.vector.tensor_copy(gx_s[:, half_cols(h)], xt_s[:].indirect(half_list(l2, h)))

        nc.vector.tensor_copy(gw_w[:].rearrange("p (t q) -> p q t", t=PACK), wt_w[:].indirect(l1[:]))
        nc.vector.tensor_copy(gw_s[:].rearrange("p (t q) -> p q t", t=PACK), wt_s[:].indirect(l1[:]))
        gather_x(0)

        def first_product(acc, t, cols):
            rows = slice(t * P, (t + 1) * P)
            nc.tensor.matmul_mx(out=acc, lhsT=gw_w[:, rows].bitcast(FP8X4), lhsT_scale=gw_s[:, rows],
                                rhs=gx_w[:, cols].bitcast(FP4X4), rhs_scale=gx_s[:, cols], start=True, stop=True)

        a = [sb.tile([P, J], F32, name="a%d" % t) for t in range(PACK)]
        acc00 = ps.tile([P, HALF], F32, name="acc00")
        first_product(acc00[:], 0, half_cols(0))
        nc.scalar.copy(a[0][:, half_cols(0)], acc00[:])
        nc.scalar.activation(board[0][:].indirect(half_list(l3, 0)), a[0][:, half_cols(0)], ACT.Copy)
        gather_x(1)
        acc01 = ps.tile([P, HALF], F32, name="acc01")
        first_product(acc01[:], 0, half_cols(1))
        nc.vector.tensor_copy(a[0][:, half_cols(1)], acc01[:])
        nc.scalar.activation(board[0][:].indirect(half_list(l3, 1)), a[0][:, half_cols(1)], ACT.Copy)
        for t in range(1, PACK):
            acc = ps.tile([P, J], F32, name="acc%d" % t)
            first_product(acc[:], t, slice(0, J))
            nc.vector.tensor_copy(a[t][:], acc[:])
            nc.scalar.activation(board[t][:].indirect(l3[:]), a[t][:], ACT.Copy)

        diff = [sb.tile([P, 2, 2, J], F32, name="diff0", tag="gw_w", align_bytes=64), sb.tile([P, 2, 2, J], F32, name="diff1")]
        mag = sb.tile([P, 2, 2, J, 2], F32, name="mag")
        for t in range(PACK - 1):
            for w, lst in enumerate((l4, l5)):
                nc.vector.tensor_tensor(diff[t // 2][:, w, t % 2, :], board[t][:].indirect(lst[:]), a[t][:], ALU.subtract)
        nc.scalar.activation(mag[:, 0], diff[0][:].rearrange("p w e j -> p w j e"), ACT.Abs)
        last = PACK - 1
        for h in range(2):
            for w, lst in enumerate((l4, l5)):
                nc.vector.tensor_tensor(diff[1][:, w, 1, half_cols(h)], board[last][:].indirect(half_list(lst, h)),
                                        a[last][:, half_cols(h)], ALU.subtract)
        for h in range(2):
            nc.scalar.activation(mag[:, 1, :, half_cols(h), :],
                                 diff[1][:, :, :, half_cols(h)].rearrange("p w e j -> p w j e"), ACT.Abs)

        for h in range(2):
            hid = sb.tile([P, HALF, 2, 2], BF16, name="hid%d" % h, align_bytes=64)
            nc.vector.tensor_tensor(hid[:], mag[:, :, 0, half_cols(h), :].rearrange("p u j e -> p j u e"),
                                    mag[:, :, 1, half_cols(h), :].rearrange("p u j e -> p j u e"), ALU.min)
            codes = sb.tile([P, HALF], U32, name="codes%d" % h, align_bytes=64)
            scales = sb.tile([P, HALF], U8, name="scales%d" % h, align_bytes=64)
            nc.vector.quantize_mx(out=codes[:].bitcast(FP8X4), scales=scales[:], in_=hid[:].rearrange("p j u e -> p (j u e)"))
            for m in range(N // P):
                rows = slice(m * P, (m + 1) * P)
                res_ps = ps.tile([P, HALF], F32, name="res_ps%d%d" % (h, m), tag="res_ps%d" % m if h == 1 else "acc0%d" % m)
                nc.tensor.matmul_mx(out=res_ps[:], lhsT=wb_w[:, rows].bitcast(FP4X4), lhsT_scale=wb_s[:, rows],
                                    rhs=codes[:].bitcast(FP8X4), rhs_scale=scales[:], start=True, stop=True)
                res = sb.tile([P, HALF], F32, name="res%d%d" % (h, m))
                if h == 1 and m == 1:
                    nc.vector.tensor_copy(res[:], res_ps[:])
                else:
                    nc.scalar.copy(res[:], res_ps[:])
                nc.sync.dma_start(out[rows, half_cols(h)], res[:])
